import numpy as np, ml_dtypes
CORES = [5,29,101,125,133,157,229,253]
N = 8
F = 128
def setup_inputs(rng):
    return {"a": rng.standard_normal((N, 128, 128), dtype=np.float32).astype(ml_dtypes.bfloat16), "w": rng.standard_normal((N, 128, F), dtype=np.float32).astype(ml_dtypes.bfloat16)}
def setup_inputs_big(rng):
    d = setup_inputs(rng)
    for k in ("a", "w"): d[k] = (d[k].astype(np.float32) * 1024.0).astype(d[k].dtype)
    return d
def setup_inputs_small(rng):
    d = setup_inputs(rng)
    for k in ("a", "w"): d[k] = (d[k].astype(np.float32) * (1 / 1024.0)).astype(d[k].dtype)
    return d
def setup_inputs_apart(rng):
    d = setup_inputs(rng)
    f = (10.0 ** rng.permutation(np.linspace(-1.5, 1.5, N))).astype(np.float32).reshape(N, 1, 1)
    for k in ("a", "w"): d[k] = (d[k].astype(np.float32) * f).astype(d[k].dtype)
    return d
def setup_inputs_neg(rng):
    d = setup_inputs(rng)
    d["a"] = (np.abs(d["a"].astype(np.float32)) * 1048576.0).astype(d["a"].dtype); d["w"] = (-np.abs(d["w"].astype(np.float32))).astype(d["w"].dtype)
    return d
def reference(a, w):
    A, W = a.astype(np.float64), w.astype(np.float64)
    p = np.stack([A[j].T @ W[j] for j in range(N)])
    return {"y": np.maximum.accumulate(p, axis=0).astype(ml_dtypes.bfloat16)}

@@ -1,0 +1,131 @@
+from concourse.bass import DstId, RemoteDMATransfer
+from concourse.mybir import AluOpType
+
+F = 128
+SLOTS = 4
+E_SEND = 8
+E_FOLD = 8
+
+SCRATCH = {
+    "a_sb": ("sbuf", [128, 128], "bfloat16"),
+    "w_sb": ("sbuf", [128, F], "bfloat16"),
+    "ps": ("psum", [128, F], "float32"),
+    "p": ("sbuf", [128, F], "bfloat16"),
+    "land": ("sbuf", [128, SLOTS * F], "bfloat16"),
+    "fin": ("sbuf", [128, 2 * F], "bfloat16"),
+    "tmp": ("sbuf", [128, SLOTS * F], "bfloat16"),
+    "out": ("sbuf", [128, F], "bfloat16"),
+}
+SEMAPHORES = ["ld", "mm", "cp", "sent", "arr", "fin", "vs", "mx", "st"]
+
+
+def _take(mask, n):
+    out, b = 0, 0
+    while n > 0:
+        assert mask >> b, "too few engines"
+        if (mask >> b) & 1:
+            out |= 1 << b
+            n -= 1
+        b += 1
+    return out
+
+
+def _slot(buf, s):
+    return buf[:, s * F:(s + 1) * F]
+
+
+def _plan(T, topo):
+    cores = list(T.cores)
+    n = len(cores)
+    world = range((max(topo.host(c) for c in cores) + 1) * topo.CORES_PER_HOST)
+    cls = [[j for j in range(k + 1) if j == k or topo.may_write(cores[j], cores[k])] for k in range(n)]
+    for k in range(1, n):
+        assert sorted(cls[k] + cls[k - 1]) == list(range(k + 1))
+    relay = {}
+    for k in range(n - 1):
+        r, d = cores[k], cores[k + 1]
+        cand = [c for c in world if c not in cores and topo.host(c) == topo.host(r) and topo.chip(c) == topo.chip(r)
+                and topo.may_write(c, d)]
+        near = [c for c in cand if topo.die(c) == topo.die(r)]
+        relay[k] = (near or cand)[0]
+    return cores, n, cls, relay
+
+
+def _write(g, T, topo, core, dests, srcs, engines, remote_sem):
+    mask = ~0
+    for d, _ in dests:
+        mask &= topo.mask(core, d)
+    ids = []
+    for d, _ in dests:
+        rid, pid = topo.addr(d, core)
+        ids.append(DstId(rid=rid, pnc=pid))
+    g.remote_dma_fused([RemoteDMATransfer(dst_ids=ids, dma_engine_mask=_take(mask, engines), remote_sem=remote_sem,
+                                          srcs=srcs, dsts=[ap for _, ap in dests], alu_op=2 if len(srcs) > 1 else 0)],
+                       local_sem=T.sem.sent)
+    g.wait_ge(T.sem.sent, engines)
+
+
+def rank_program(g, core, T, topo):
+    cores, n, cls, relay = _plan(T, topo)
+    rank = T.rank_of(core)
+
+    if rank is None:
+        for k, h in relay.items():
+            if h != core:
+                continue
+            m = len(cls[k])
+            g.wait_ge(T.sem.arr, m * E_SEND)
+            dests = [(cores[k + 1], _slot(T.fin, 1))]
+            if m > 1:
+                dests.append((cores[k], _slot(T.fin, 0)))
+            _write(g, T, topo, core, dests, [_slot(T.land, s) for s in range(m)], E_FOLD, T.sem.fin)
+        return
+
+    g.sync.dma_start(out=T.a_sb[:], in_=T.a[:]).then_inc(T.sem.ld, 16)
+    g.scalar.dma_start(out=T.w_sb[:], in_=T.w[:]).then_inc(T.sem.ld, 16)
+    g.tensor.wait_ge(T.sem.ld, 32)
+    g.tensor.matmul(T.ps[:], T.a_sb[:], T.w_sb[:], start=True, stop=True).then_inc(T.sem.mm, 1)
+    g.vector.wait_ge(T.sem.mm, 1)
+    g.vector.tensor_copy(out=T.p[:], in_=T.ps[:]).then_inc(T.sem.cp, 1)
+
+    later = [k for k in range(rank, n) if rank in cls[k]]
+    where = _slot(T.land, len(cls[rank]) - 1)
+    dests = [(relay[k], where) for k in reversed(later) if k in relay]
+    dests += [(cores[k], where) for k in later if k not in relay and k != rank]
+    g.wait_ge(T.sem.cp, 1)
+    if dests:
+        _write(g, T, topo, core, dests, [T.p[:]], E_SEND, T.sem.arr)
+
+    back = rank in relay and len(cls[rank]) > 1
+    early, late = [], []
+    if not back:
+        early = [T.p[:]] + [_slot(T.land, s) for s in range(len(cls[rank]) - 1)]
+    else:
+        late.append(_slot(T.fin, 0))
+    if rank > 0:
+        late.append(_slot(T.fin, 1))
+    tiles = early + late
+
+    if len(tiles) == 1:
+        res = tiles[0]
+        g.sync.wait_ge(T.sem.cp, 1)
+    else:
+        if early:
+            g.vector.wait_ge(T.sem.cp, 1)
+        if len(early) > 1:
+            g.vector.wait_ge(T.sem.arr, (len(early) - 1) * E_SEND)
+        acc = tiles[0]
+        for i in range(1, len(tiles)):
+            if i == max(len(early), 1):
+                g.vector.wait_ge(T.sem.fin, len(late) * E_FOLD)
+            if i > 1:
+                g.vector.wait_ge(T.sem.vs, i - 1)
+            last = i == len(tiles) - 1
+            dst = T.out[:] if last else _slot(T.tmp, i - 1)
+            g.vector.tensor_tensor(out=dst, in0=acc, in1=tiles[i], op=AluOpType.max).then_inc(
+                T.sem.mx if last else T.sem.vs, 1)
+            acc = dst
+        res = T.out[:]
+        g.sync.wait_ge(T.sem.mx, 1)
+    g.sync.dma_start(out=T.y[:], in_=res).then_inc(T.sem.st, 16)
+    g.sync.wait_ge(T.sem.st, 16)

@@ -2,21 +2,20 @@ from concourse.bass import DstId, RemoteDMATransfer
 from concourse.mybir import AluOpType
 
 F = 128
-SLOTS = 4
-E_SEND = 8
-E_FOLD = 8
+E = 8
+DUAL = True
 
 SCRATCH = {
     "a_sb": ("sbuf", [128, 128], "bfloat16"),
     "w_sb": ("sbuf", [128, F], "bfloat16"),
     "ps": ("psum", [128, F], "float32"),
     "p": ("sbuf", [128, F], "bfloat16"),
-    "land": ("sbuf", [128, SLOTS * F], "bfloat16"),
+    "land": ("sbuf", [128, 2 * F], "bfloat16"),
+    "dirt": ("sbuf", [128, 3 * F], "bfloat16"),
     "fin": ("sbuf", [128, 2 * F], "bfloat16"),
-    "tmp": ("sbuf", [128, SLOTS * F], "bfloat16"),
     "out": ("sbuf", [128, F], "bfloat16"),
 }
-SEMAPHORES = ["ld", "mm", "cp", "sent", "arr", "fin", "vs", "mx", "st"]
+SEMAPHORES = ["ld", "mm", "cp", "sent", "h0", "h1", "h2", "h3", "l0", "l1", "vs", "mx", "st"]
 
 
 def _take(mask, n):
@@ -34,52 +33,78 @@ def _slot(buf, s):
     return buf[:, s * F:(s + 1) * F]
 
 
+def _same_chip(topo, a, b):
+    return topo.host(a) == topo.host(b) and topo.chip(a) == topo.chip(b)
+
+
 def _plan(T, topo):
     cores = list(T.cores)
     n = len(cores)
     world = range((max(topo.host(c) for c in cores) + 1) * topo.CORES_PER_HOST)
-    cls = [[j for j in range(k + 1) if j == k or topo.may_write(cores[j], cores[k])] for k in range(n)]
-    for k in range(1, n):
-        assert sorted(cls[k] + cls[k - 1]) == list(range(k + 1))
-    relay = {}
-    for k in range(n - 1):
-        r, d = cores[k], cores[k + 1]
-        cand = [c for c in world if c not in cores and topo.host(c) == topo.host(r) and topo.chip(c) == topo.chip(r)
-                and topo.may_write(c, d)]
-        near = [c for c in cand if topo.die(c) == topo.die(r)]
-        relay[k] = (near or cand)[0]
-    return cores, n, cls, relay
+    classes = []
+    for r in range(n):
+        for L in classes:
+            if topo.may_write(cores[L[0]], cores[r]) and topo.may_write(cores[r], cores[L[0]]):
+                L.append(r)
+                break
+        else:
+            classes.append([r])
+    assert len(classes) == 2
+    place = {r: (c, L.index(r)) for c, L in enumerate(classes) for r in L}
+    dests = {}
+    for k in range(n):
+        o = 1 - place[k][0]
+        m = len([j for j in classes[o] if j < k])
+        for i in range(m - 1, -1, -2):
+            dests.setdefault((o, i), []).append(k)
+    relays = {}
+    for (c, i), ds in dests.items():
+        r = cores[classes[c][i]]
+        cand = [x for x in world if x not in cores and _same_chip(topo, x, r)
+                and all(topo.may_write(x, cores[d]) for d in ds)]
+        near = [x for x in cand if topo.die(x) == topo.die(r)]
+        relays[(c, i)] = [(near or cand)[0], ds]
+    return cores, classes, place, relays
 
 
-def _write(g, T, topo, core, dests, srcs, engines, remote_sem):
-    mask = ~0
-    for d, _ in dests:
-        mask &= topo.mask(core, d)
+def _transfer(topo, core, dests, srcs, mask, remote_sem):
     ids = []
     for d, _ in dests:
         rid, pid = topo.addr(d, core)
         ids.append(DstId(rid=rid, pnc=pid))
-    g.remote_dma_fused([RemoteDMATransfer(dst_ids=ids, dma_engine_mask=_take(mask, engines), remote_sem=remote_sem,
-                                          srcs=srcs, dsts=[ap for _, ap in dests], alu_op=2 if len(srcs) > 1 else 0)],
-                       local_sem=T.sem.sent)
-    g.wait_ge(T.sem.sent, engines)
+    return RemoteDMATransfer(dst_ids=ids, dma_engine_mask=mask, remote_sem=remote_sem, srcs=srcs,
+                             dsts=[ap for _, ap in dests], alu_op=2 if len(srcs) > 1 else 0)
+
+
+def _common(topo, core, dests):
+    mask = ~0
+    for d, _ in dests:
+        mask &= topo.mask(core, d)
+    return mask
 
 
 def rank_program(g, core, T, topo):
-    cores, n, cls, relay = _plan(T, topo)
+    cores, classes, place, relays = _plan(T, topo)
     rank = T.rank_of(core)
 
     if rank is None:
-        for k, h in relay.items():
+        for (c, i), (h, ds) in relays.items():
             if h != core:
                 continue
-            m = len(cls[k])
-            g.wait_ge(T.sem.arr, m * E_SEND)
-            dests = [(cores[k + 1], _slot(T.fin, 1))]
-            if m > 1:
-                dests.append((cores[k], _slot(T.fin, 0)))
-            _write(g, T, topo, core, dests, [_slot(T.land, s) for s in range(m)], E_FOLD, T.sem.fin)
+            srcs = [_slot(T.land, 0)]
+            g.wait_ge(T.sem["h%d" % i], E)
+            if i > 0:
+                srcs.append(_slot(T.land, 1))
+                g.wait_ge(T.sem["h%d" % (i - 1)], E)
+            s = (i // 2) % 2
+            dd = [(cores[d], _slot(T.fin, s)) for d in ds]
+            g.remote_dma_fused([_transfer(topo, core, dd, srcs, _take(_common(topo, core, dd), E), T.sem["l%d" % s])],
+                               local_sem=T.sem.sent)
+            g.wait_ge(T.sem.sent, E)
         return
+
+    c, i = place[rank]
+    L = classes[c]
 
     g.sync.dma_start(out=T.a_sb[:], in_=T.a[:]).then_inc(T.sem.ld, 16)
     g.scalar.dma_start(out=T.w_sb[:], in_=T.w[:]).then_inc(T.sem.ld, 16)
@@ -88,44 +113,43 @@ def rank_program(g, core, T, topo):
     g.vector.wait_ge(T.sem.mm, 1)
     g.vector.tensor_copy(out=T.p[:], in_=T.ps[:]).then_inc(T.sem.cp, 1)
 
-    later = [k for k in range(rank, n) if rank in cls[k]]
-    where = _slot(T.land, len(cls[rank]) - 1)
-    dests = [(relay[k], where) for k in reversed(later) if k in relay]
-    dests += [(cores[k], where) for k in later if k not in relay and k != rank]
+    far, near = [], []
+    if (c, i + 1) in relays:
+        far.append((relays[(c, i + 1)][0], _slot(T.land, 1)))
+    if (c, i) in relays:
+        near.append((relays[(c, i)][0], _slot(T.land, 0)))
+    direct = [(cores[k], _slot(T.dirt, i)) for k in L[i + 1:]]
+    sem = T.sem["h%d" % i]
+    groups = [far + direct, near] if DUAL else [far + near + direct]
+    groups = [x for x in groups if x]
     g.wait_ge(T.sem.cp, 1)
-    if dests:
-        _write(g, T, topo, core, dests, [T.p[:]], E_SEND, T.sem.arr)
+    if groups:
+        used, trs = 0, []
+        for x in groups:
+            m = _take(_common(topo, core, x) & ~used, E)
+            used |= m
+            trs.append(_transfer(topo, core, x, [T.p[:]], m, sem))
+        g.remote_dma_fused(trs, local_sem=T.sem.sent)
 
-    back = rank in relay and len(cls[rank]) > 1
-    early, late = [], []
-    if not back:
-        early = [T.p[:]] + [_slot(T.land, s) for s in range(len(cls[rank]) - 1)]
-    else:
-        late.append(_slot(T.fin, 0))
-    if rank > 0:
-        late.append(_slot(T.fin, 1))
-    tiles = early + late
+    m = len([j for j in classes[1 - c] if j < rank])
+    tiles = [(_slot(T.dirt, j), T.sem["h%d" % j]) for j in range(i - 1, -1, -1)]
+    tiles += [(_slot(T.fin, (j // 2) % 2), T.sem["l%d" % ((j // 2) % 2)]) for j in range(m - 1, -1, -2)]
 
-    if len(tiles) == 1:
-        res = tiles[0]
+    if not tiles:
+        res = T.p[:]
         g.sync.wait_ge(T.sem.cp, 1)
     else:
-        if early:
-            g.vector.wait_ge(T.sem.cp, 1)
-        if len(early) > 1:
-            g.vector.wait_ge(T.sem.arr, (len(early) - 1) * E_SEND)
-        acc = tiles[0]
-        for i in range(1, len(tiles)):
-            if i == max(len(early), 1):
-                g.vector.wait_ge(T.sem.fin, len(late) * E_FOLD)
-            if i > 1:
-                g.vector.wait_ge(T.sem.vs, i - 1)
-            last = i == len(tiles) - 1
-            dst = T.out[:] if last else _slot(T.tmp, i - 1)
-            g.vector.tensor_tensor(out=dst, in0=acc, in1=tiles[i], op=AluOpType.max).then_inc(
+        g.vector.wait_ge(T.sem.cp, 1)
+        for t, (ap, s) in enumerate(tiles):
+            g.vector.wait_ge(s, E)
+            if t > 0:
+                g.vector.wait_ge(T.sem.vs, t)
+            last = t == len(tiles) - 1
+            g.vector.tensor_tensor(out=T.out[:] if last else T.ps[:], in0=T.ps[:], in1=ap, op=AluOpType.max).then_inc(
                 T.sem.mx if last else T.sem.vs, 1)
-            acc = dst
         res = T.out[:]
         g.sync.wait_ge(T.sem.mx, 1)
     g.sync.dma_start(out=T.y[:], in_=res).then_inc(T.sem.st, 16)
+    if groups:
+        g.wait_ge(T.sem.sent, E * len(groups))
     g.sync.wait_ge(T.sem.st, 16)

from concourse.bass import DstId, RemoteDMATransfer
from concourse.mybir import AluOpType

F = 128
E = 8
DUAL = True

SCRATCH = {
    "a_sb": ("sbuf", [128, 128], "bfloat16"),
    "w_sb": ("sbuf", [128, F], "bfloat16"),
    "ps": ("psum", [128, F], "float32"),
    "p": ("sbuf", [128, F], "bfloat16"),
    "land": ("sbuf", [128, 2 * F], "bfloat16"),
    "dirt": ("sbuf", [128, 3 * F], "bfloat16"),
    "fin": ("sbuf", [128, 2 * F], "bfloat16"),
    "out": ("sbuf", [128, F], "bfloat16"),
}
SEMAPHORES = ["ld", "mm", "cp", "sent", "h0", "h1", "h2", "h3", "l0", "l1", "vs", "mx", "st"]


def _take(mask, n):
    out, b = 0, 0
    while n > 0:
        assert mask >> b, "too few engines"
        if (mask >> b) & 1:
            out |= 1 << b
            n -= 1
        b += 1
    return out


def _slot(buf, s):
    return buf[:, s * F:(s + 1) * F]


def _same_chip(topo, a, b):
    return topo.host(a) == topo.host(b) and topo.chip(a) == topo.chip(b)


def _plan(T, topo):
    cores = list(T.cores)
    n = len(cores)
    world = range((max(topo.host(c) for c in cores) + 1) * topo.CORES_PER_HOST)
    classes = []
    for r in range(n):
        for L in classes:
            if topo.may_write(cores[L[0]], cores[r]) and topo.may_write(cores[r], cores[L[0]]):
                L.append(r)
                break
        else:
            classes.append([r])
    assert len(classes) == 2
    place = {r: (c, L.index(r)) for c, L in enumerate(classes) for r in L}
    dests = {}
    for k in range(n):
        o = 1 - place[k][0]
        m = len([j for j in classes[o] if j < k])
        for i in range(m - 1, -1, -2):
            dests.setdefault((o, i), []).append(k)
    relays = {}
    for (c, i), ds in dests.items():
        r = cores[classes[c][i]]
        cand = [x for x in world if x not in cores and _same_chip(topo, x, r)
                and all(topo.may_write(x, cores[d]) for d in ds)]
        near = [x for x in cand if topo.die(x) == topo.die(r)]
        relays[(c, i)] = [(near or cand)[0], ds]
    return cores, classes, place, relays


def _transfer(topo, core, dests, srcs, mask, remote_sem):
    ids = []
    for d, _ in dests:
        rid, pid = topo.addr(d, core)
        ids.append(DstId(rid=rid, pnc=pid))
    return RemoteDMATransfer(dst_ids=ids, dma_engine_mask=mask, remote_sem=remote_sem, srcs=srcs,
                             dsts=[ap for _, ap in dests], alu_op=2 if len(srcs) > 1 else 0)


def _common(topo, core, dests):
    mask = ~0
    for d, _ in dests:
        mask &= topo.mask(core, d)
    return mask


def rank_program(g, core, T, topo):
    cores, classes, place, relays = _plan(T, topo)
    rank = T.rank_of(core)

    if rank is None:
        for (c, i), (h, ds) in relays.items():
            if h != core:
                continue
            srcs = [_slot(T.land, 0)]
            g.wait_ge(T.sem["h%d" % i], E)
            if i > 0:
                srcs.append(_slot(T.land, 1))
                g.wait_ge(T.sem["h%d" % (i - 1)], E)
            s = (i // 2) % 2
            dd = [(cores[d], _slot(T.fin, s)) for d in ds]
            g.remote_dma_fused([_transfer(topo, core, dd, srcs, _take(_common(topo, core, dd), E), T.sem["l%d" % s])],
                               local_sem=T.sem.sent)
            g.wait_ge(T.sem.sent, E)
        return

    c, i = place[rank]
    L = classes[c]

    g.sync.dma_start(out=T.a_sb[:], in_=T.a[:]).then_inc(T.sem.ld, 16)
    g.scalar.dma_start(out=T.w_sb[:], in_=T.w[:]).then_inc(T.sem.ld, 16)
    g.tensor.wait_ge(T.sem.ld, 32)
    g.tensor.matmul(T.ps[:], T.a_sb[:], T.w_sb[:], start=True, stop=True).then_inc(T.sem.mm, 1)
    g.vector.wait_ge(T.sem.mm, 1)
    g.vector.tensor_copy(out=T.p[:], in_=T.ps[:]).then_inc(T.sem.cp, 1)

    far, near = [], []
    if (c, i + 1) in relays:
        far.append((relays[(c, i + 1)][0], _slot(T.land, 1)))
    if (c, i) in relays:
        near.append((relays[(c, i)][0], _slot(T.land, 0)))
    direct = [(cores[k], _slot(T.dirt, i)) for k in L[i + 1:]]
    sem = T.sem["h%d" % i]
    groups = [far + direct, near] if DUAL else [far + near + direct]
    groups = [x for x in groups if x]
    g.wait_ge(T.sem.cp, 1)
    if groups:
        used, trs = 0, []
        for x in groups:
            m = _take(_common(topo, core, x) & ~used, E)
            used |= m
            trs.append(_transfer(topo, core, x, [T.p[:]], m, sem))
        g.remote_dma_fused(trs, local_sem=T.sem.sent)

    m = len([j for j in classes[1 - c] if j < rank])
    tiles = [(_slot(T.dirt, j), T.sem["h%d" % j]) for j in range(i - 1, -1, -1)]
    tiles += [(_slot(T.fin, (j // 2) % 2), T.sem["l%d" % ((j // 2) % 2)]) for j in range(m - 1, -1, -2)]

    if not tiles:
        res = T.p[:]
        g.sync.wait_ge(T.sem.cp, 1)
    else:
        g.vector.wait_ge(T.sem.cp, 1)
        for t, (ap, s) in enumerate(tiles):
            g.vector.wait_ge(s, E)
            if t > 0:
                g.vector.wait_ge(T.sem.vs, t)
            last = t == len(tiles) - 1
            g.vector.tensor_tensor(out=T.out[:] if last else T.ps[:], in0=T.ps[:], in1=ap, op=AluOpType.max).then_inc(
                T.sem.mx if last else T.sem.vs, 1)
        res = T.out[:]
        g.sync.wait_ge(T.sem.mx, 1)
    g.sync.dma_start(out=T.y[:], in_=res).then_inc(T.sem.st, 16)
    if groups:
        g.wait_ge(T.sem.sent, E * len(groups))
    g.sync.wait_ge(T.sem.st, 16)
